import numpy as np
import ml_dtypes

BF16 = ml_dtypes.bfloat16


def bf(x):
    return np.asarray(x, np.float32).astype(BF16)


def f32(x):
    return np.asarray(x, np.float32)


def f64(x):
    return np.asarray(x).astype(np.float64)


def striped(idx):
    return np.tile(idx.reshape(-1, 16).T, (8, 1))


S, K, M, N, D, V = 1024, 128, 256, 1536, 2, 768


def setup_inputs():
    return {"table": bf(np.random.standard_normal((S, K))), "w": bf(np.random.standard_normal((D, K, M)) / np.sqrt(D * K)), "b": f32(0.5 * np.random.standard_normal((M, 1))), "offs": striped(np.random.permutation(np.tile(np.arange(S), 2))[:N])}


def reference(table, w, b, offs):
    idx = offs[:16].T.reshape(-1)
    x = f64(table)[idx].T
    y = sum(f64(w)[t].T @ x[:, t * V : (t + 1) * V] for t in range(D))
    return y + f64(b)

@@ -1,0 +1,78 @@
+import concourse.mybir as mybir
+from concourse.masks import make_identity
+
+BF16, F32, U16 = mybir.dt.bfloat16, mybir.dt.float32, mybir.dt.uint16
+IDENTITY = mybir.ActivationFunctionType.Identity
+
+P = 128
+NODES = 1024
+ENDS = 2
+EDGES = 768
+FEATURES_OUT = 256
+PIECE = 384
+PER_COLUMN = 16
+BLOCKS_PER_LOAD = 2
+
+FLOPS = 2 * ENDS * P * FEATURES_OUT * EDGES
+
+
+def tile_gather_matmul_kernel(tc, table, w, b, offs, out):
+    nc = tc.nc
+    nodes_per_load = BLOCKS_PER_LOAD * P
+    n_loads = NODES // nodes_per_load
+    with (
+        tc.tile_pool(name="held", bufs=1) as held,
+        tc.tile_pool(name="results", bufs=4) as results,
+        tc.psum_pool(name="flips", bufs=2) as flips,
+        tc.psum_pool(name="sums", bufs=4) as sums,
+    ):
+        offsets = held.tile([P, ENDS * EDGES // PER_COLUMN], U16, name="offsets")
+        nc.sync.dma_start(offsets[:], offs)
+        node_rows = []
+        for part in range(n_loads):
+            rows = held.tile([P, BLOCKS_PER_LOAD, P], BF16, name="rows%d" % part)
+            queue = nc.sync if part % 2 == 0 else nc.scalar
+            queue.dma_start(
+                rows[:],
+                table[part * nodes_per_load : (part + 1) * nodes_per_load, :].rearrange("(a p) k -> p a k", p=P),
+            )
+            node_rows.append(rows)
+        weights = held.tile([P, ENDS, FEATURES_OUT], BF16, name="weights")
+        nc.sync.dma_start(weights[:], w.rearrange("t k m -> k t m"))
+        bias = held.tile([P, FEATURES_OUT // P], F32, name="bias")
+        with nc.allow_non_contiguous_dma(reason="one float32 of the bias to a partition"):
+            nc.scalar.dma_start(bias[:], b.rearrange("(a p) o -> p (a o)", p=P))
+
+        identity = held.tile([P, P], BF16, name="identity")
+        make_identity(nc, identity[:])
+        window = held.tile([P, NODES], BF16, name="window")
+        for part in range(n_loads):
+            flipped = flips.tile([P, nodes_per_load], BF16, name="flipped")
+            for a in range(BLOCKS_PER_LOAD):
+                nc.tensor.transpose(flipped[:, a * P : (a + 1) * P], node_rows[part][:, a, :], identity[:])
+            columns = window[:, part * nodes_per_load : (part + 1) * nodes_per_load]
+            if part % 2 == 0:
+                nc.vector.tensor_copy(columns, flipped[:])
+            else:
+                nc.scalar.copy(columns, flipped[:])
+
+        for m_block in range(FEATURES_OUT // P):
+            for piece in range(EDGES // PIECE):
+                total = sums.tile([P, PIECE], F32, name="total")
+                for end in range(ENDS):
+                    first = (end * EDGES + piece * PIECE) // PER_COLUMN
+                    nc.tensor.matmul(
+                        total[:],
+                        weights[:, end, m_block * P : (m_block + 1) * P],
+                        window[:].indirect(offsets[:, first : first + PIECE // PER_COLUMN]),
+                        start=(end == 0),
+                        stop=(end == ENDS - 1),
+                    )
+                result = results.tile([P, PIECE], F32, name="result")
+                target = out[m_block * P : (m_block + 1) * P, piece * PIECE : (piece + 1) * PIECE]
+                if piece % 2 == 0:
+                    nc.vector.tensor_scalar_add(result[:], total[:], bias[:, m_block : m_block + 1])
+                    nc.sync.dma_start(target, result[:])
+                else:
+                    nc.scalar.activation(result[:], total[:], IDENTITY, bias=bias[:, m_block : m_block + 1])
+                    nc.scalar.dma_start(target, result[:])

@@ -12,6 +12,8 @@ FEATURES_OUT = 256
 PIECE = 384
 PER_COLUMN = 16
 BLOCKS_PER_LOAD = 2
+BANK = 512
+WARM_UP = 4
 
 FLOPS = 2 * ENDS * P * FEATURES_OUT * EDGES
 
@@ -25,7 +27,14 @@ def tile_gather_matmul_kernel(tc, table, w, b, offs, out):
         tc.tile_pool(name="results", bufs=4) as results,
         tc.psum_pool(name="flips", bufs=2) as flips,
         tc.psum_pool(name="sums", bufs=4) as sums,
+        tc.psum_pool(name="unused", bufs=1) as unused,
     ):
+        zeros = held.tile([P, BANK], BF16, name="zeros")
+        nc.vector.memset(zeros[:], 0.0)
+        nothing = unused.tile([P, BANK], F32, name="nothing")
+        for i in range(WARM_UP):
+            nc.tensor.matmul(nothing[:], zeros[:, :P], zeros[:], start=True, stop=True)
+
         offsets = held.tile([P, ENDS * EDGES // PER_COLUMN], U16, name="offsets")
         nc.sync.dma_start(offsets[:], offs)
         node_rows = []

@@ -2,7 +2,6 @@ import concourse.mybir as mybir
 from concourse.masks import make_identity
 
 BF16, F32, U16 = mybir.dt.bfloat16, mybir.dt.float32, mybir.dt.uint16
-IDENTITY = mybir.ActivationFunctionType.Identity
 
 P = 128
 NODES = 1024
@@ -13,7 +12,8 @@ PIECE = 384
 PER_COLUMN = 16
 BLOCKS_PER_LOAD = 2
 BANK = 512
-WARM_UP = 4
+WARM_UP = 2
+BRIDGE = 2
 
 FLOPS = 2 * ENDS * P * FEATURES_OUT * EDGES
 
@@ -25,18 +25,10 @@ def tile_gather_matmul_kernel(tc, table, w, b, offs, out):
     with (
         tc.tile_pool(name="held", bufs=1) as held,
         tc.tile_pool(name="results", bufs=4) as results,
-        tc.psum_pool(name="flips", bufs=2) as flips,
+        tc.psum_pool(name="flips", bufs=3) as flips,
         tc.psum_pool(name="sums", bufs=4) as sums,
         tc.psum_pool(name="unused", bufs=1) as unused,
     ):
-        zeros = held.tile([P, BANK], BF16, name="zeros")
-        nc.vector.memset(zeros[:], 0.0)
-        nothing = unused.tile([P, BANK], F32, name="nothing")
-        for i in range(WARM_UP):
-            nc.tensor.matmul(nothing[:], zeros[:, :P], zeros[:], start=True, stop=True)
-
-        offsets = held.tile([P, ENDS * EDGES // PER_COLUMN], U16, name="offsets")
-        nc.sync.dma_start(offsets[:], offs)
         node_rows = []
         for part in range(n_loads):
             rows = held.tile([P, BLOCKS_PER_LOAD, P], BF16, name="rows%d" % part)
@@ -46,11 +38,23 @@ def tile_gather_matmul_kernel(tc, table, w, b, offs, out):
                 table[part * nodes_per_load : (part + 1) * nodes_per_load, :].rearrange("(a p) k -> p a k", p=P),
             )
             node_rows.append(rows)
+        offsets = held.tile([P, ENDS * EDGES // PER_COLUMN], U16, name="offsets")
+        nc.sync.dma_start(offsets[:], offs)
         weights = held.tile([P, ENDS, FEATURES_OUT], BF16, name="weights")
-        nc.sync.dma_start(weights[:], w.rearrange("t k m -> k t m"))
+        nc.scalar.dma_start(weights[:], w.rearrange("t k m -> k t m"))
         bias = held.tile([P, FEATURES_OUT // P], F32, name="bias")
         with nc.allow_non_contiguous_dma(reason="one float32 of the bias to a partition"):
-            nc.scalar.dma_start(bias[:], b.rearrange("(a p) o -> p (a o)", p=P))
+            nc.sync.dma_start(bias[:], b.rearrange("(a p) o -> p (a o)", p=P))
+
+        zeros = held.tile([P, BANK], BF16, name="zeros")
+        nc.vector.memset(zeros[:], 0.0)
+        nothing = unused.tile([P, BANK], F32, name="nothing")
+
+        def multiply_zeros(times):
+            for i in range(times):
+                nc.tensor.matmul(nothing[:], zeros[:, :P], zeros[:], start=True, stop=True)
+
+        multiply_zeros(WARM_UP)
 
         identity = held.tile([P, P], BF16, name="identity")
         make_identity(nc, identity[:])
@@ -59,11 +63,8 @@ def tile_gather_matmul_kernel(tc, table, w, b, offs, out):
             flipped = flips.tile([P, nodes_per_load], BF16, name="flipped")
             for a in range(BLOCKS_PER_LOAD):
                 nc.tensor.transpose(flipped[:, a * P : (a + 1) * P], node_rows[part][:, a, :], identity[:])
-            columns = window[:, part * nodes_per_load : (part + 1) * nodes_per_load]
-            if part % 2 == 0:
-                nc.vector.tensor_copy(columns, flipped[:])
-            else:
-                nc.scalar.copy(columns, flipped[:])
+            nc.vector.tensor_copy(window[:, part * nodes_per_load : (part + 1) * nodes_per_load], flipped[:])
+        multiply_zeros(BRIDGE)
 
         for m_block in range(FEATURES_OUT // P):
             for piece in range(EDGES // PIECE):
@@ -78,10 +79,6 @@ def tile_gather_matmul_kernel(tc, table, w, b, offs, out):
                         stop=(end == ENDS - 1),
                     )
                 result = results.tile([P, PIECE], F32, name="result")
-                target = out[m_block * P : (m_block + 1) * P, piece * PIECE : (piece + 1) * PIECE]
-                if piece % 2 == 0:
-                    nc.vector.tensor_scalar_add(result[:], total[:], bias[:, m_block : m_block + 1])
-                    nc.sync.dma_start(target, result[:])
-                else:
-                    nc.scalar.activation(result[:], total[:], IDENTITY, bias=bias[:, m_block : m_block + 1])
-                    nc.scalar.dma_start(target, result[:])
+                nc.vector.tensor_scalar_add(result[:], total[:], bias[:, m_block : m_block + 1])
+                queue = nc.sync if piece % 2 == 0 else nc.scalar
+                queue.dma_start(out[m_block * P : (m_block + 1) * P, piece * PIECE : (piece + 1) * PIECE], result[:])

@@ -11,9 +11,6 @@ FEATURES_OUT = 256
 PIECE = 384
 PER_COLUMN = 16
 BLOCKS_PER_LOAD = 2
-BANK = 512
-WARM_UP = 2
-BRIDGE = 2
 
 FLOPS = 2 * ENDS * P * FEATURES_OUT * EDGES
 
@@ -27,7 +24,6 @@ def tile_gather_matmul_kernel(tc, table, w, b, offs, out):
         tc.tile_pool(name="results", bufs=4) as results,
         tc.psum_pool(name="flips", bufs=3) as flips,
         tc.psum_pool(name="sums", bufs=4) as sums,
-        tc.psum_pool(name="unused", bufs=1) as unused,
     ):
         node_rows = []
         for part in range(n_loads):
@@ -46,16 +42,6 @@ def tile_gather_matmul_kernel(tc, table, w, b, offs, out):
         with nc.allow_non_contiguous_dma(reason="one float32 of the bias to a partition"):
             nc.sync.dma_start(bias[:], b.rearrange("(a p) o -> p (a o)", p=P))
 
-        zeros = held.tile([P, BANK], BF16, name="zeros")
-        nc.vector.memset(zeros[:], 0.0)
-        nothing = unused.tile([P, BANK], F32, name="nothing")
-
-        def multiply_zeros(times):
-            for i in range(times):
-                nc.tensor.matmul(nothing[:], zeros[:, :P], zeros[:], start=True, stop=True)
-
-        multiply_zeros(WARM_UP)
-
         identity = held.tile([P, P], BF16, name="identity")
         make_identity(nc, identity[:])
         window = held.tile([P, NODES], BF16, name="window")
@@ -64,7 +50,6 @@ def tile_gather_matmul_kernel(tc, table, w, b, offs, out):
             for a in range(BLOCKS_PER_LOAD):
                 nc.tensor.transpose(flipped[:, a * P : (a + 1) * P], node_rows[part][:, a, :], identity[:])
             nc.vector.tensor_copy(window[:, part * nodes_per_load : (part + 1) * nodes_per_load], flipped[:])
-        multiply_zeros(BRIDGE)
 
         for m_block in range(FEATURES_OUT // P):
             for piece in range(EDGES // PIECE):

@@ -9,6 +9,7 @@ ENDS = 2
 EDGES = 768
 FEATURES_OUT = 256
 PIECE = 384
+HALF = PIECE // 2
 PER_COLUMN = 16
 BLOCKS_PER_LOAD = 2
 
@@ -21,7 +22,7 @@ def tile_gather_matmul_kernel(tc, table, w, b, offs, out):
     n_loads = NODES // nodes_per_load
     with (
         tc.tile_pool(name="held", bufs=1) as held,
-        tc.tile_pool(name="results", bufs=4) as results,
+        tc.tile_pool(name="results", bufs=8) as results,
         tc.psum_pool(name="flips", bufs=3) as flips,
         tc.psum_pool(name="sums", bufs=4) as sums,
     ):
@@ -63,7 +64,11 @@ def tile_gather_matmul_kernel(tc, table, w, b, offs, out):
                         start=(end == 0),
                         stop=(end == ENDS - 1),
                     )
-                result = results.tile([P, PIECE], F32, name="result")
-                nc.vector.tensor_scalar_add(result[:], total[:], bias[:, m_block : m_block + 1])
-                queue = nc.sync if piece % 2 == 0 else nc.scalar
-                queue.dma_start(out[m_block * P : (m_block + 1) * P, piece * PIECE : (piece + 1) * PIECE], result[:])
+                for half in range(PIECE // HALF):
+                    result = results.tile([P, HALF], F32, name="result")
+                    nc.vector.tensor_scalar_add(
+                        result[:], total[:, half * HALF : (half + 1) * HALF], bias[:, m_block : m_block + 1]
+                    )
+                    first_edge = piece * PIECE + half * HALF
+                    queue = nc.sync if half % 2 == 0 else nc.scalar
+                    queue.dma_start(out[m_block * P : (m_block + 1) * P, first_edge : first_edge + HALF], result[:])

@@ -24,7 +24,7 @@ def tile_gather_matmul_kernel(tc, table, w, b, offs, out):
         tc.tile_pool(name="held", bufs=1) as held,
         tc.tile_pool(name="results", bufs=8) as results,
         tc.psum_pool(name="flips", bufs=3) as flips,
-        tc.psum_pool(name="sums", bufs=4) as sums,
+        tc.psum_pool(name="sums", bufs=5) as sums,
     ):
         node_rows = []
         for part in range(n_loads):
@@ -52,23 +52,27 @@ def tile_gather_matmul_kernel(tc, table, w, b, offs, out):
                 nc.tensor.transpose(flipped[:, a * P : (a + 1) * P], node_rows[part][:, a, :], identity[:])
             nc.vector.tensor_copy(window[:, part * nodes_per_load : (part + 1) * nodes_per_load], flipped[:])
 
-        for m_block in range(FEATURES_OUT // P):
-            for piece in range(EDGES // PIECE):
-                total = sums.tile([P, PIECE], F32, name="total")
-                for end in range(ENDS):
-                    first = (end * EDGES + piece * PIECE) // PER_COLUMN
-                    nc.tensor.matmul(
-                        total[:],
-                        weights[:, end, m_block * P : (m_block + 1) * P],
-                        window[:].indirect(offsets[:, first : first + PIECE // PER_COLUMN]),
-                        start=(end == 0),
-                        stop=(end == ENDS - 1),
-                    )
-                for half in range(PIECE // HALF):
-                    result = results.tile([P, HALF], F32, name="result")
-                    nc.vector.tensor_scalar_add(
-                        result[:], total[:, half * HALF : (half + 1) * HALF], bias[:, m_block : m_block + 1]
-                    )
-                    first_edge = piece * PIECE + half * HALF
-                    queue = nc.sync if half % 2 == 0 else nc.scalar
-                    queue.dma_start(out[m_block * P : (m_block + 1) * P, first_edge : first_edge + HALF], result[:])
+        spans = [(m_block, first_edge, PIECE) for m_block in range(FEATURES_OUT // P) for first_edge in range(0, EDGES, PIECE)]
+        last_block, last_first, last_width = spans.pop()
+        spans.extend((last_block, last_first + half * HALF, HALF) for half in range(last_width // HALF))
+
+        n_stores = 0
+        for m_block, first_edge, width in spans:
+            total = sums.tile([P, width], F32, name="total")
+            for end in range(ENDS):
+                first = (end * EDGES + first_edge) // PER_COLUMN
+                nc.tensor.matmul(
+                    total[:],
+                    weights[:, end, m_block * P : (m_block + 1) * P],
+                    window[:].indirect(offsets[:, first : first + width // PER_COLUMN]),
+                    start=(end == 0),
+                    stop=(end == ENDS - 1),
+                )
+            for column in range(0, width, HALF):
+                result = results.tile([P, HALF], F32, name="result")
+                nc.vector.tensor_scalar_add(result[:], total[:, column : column + HALF], bias[:, m_block : m_block + 1])
+                queue = nc.sync if n_stores % 2 == 0 else nc.scalar
+                queue.dma_start(
+                    out[m_block * P : (m_block + 1) * P, first_edge + column : first_edge + column + HALF], result[:]
+                )
+                n_stores += 1

@@ -12,6 +12,8 @@ PIECE = 384
 HALF = PIECE // 2
 PER_COLUMN = 16
 BLOCKS_PER_LOAD = 2
+WARM_UPS = 3
+WARM_COLUMNS = 512
 
 FLOPS = 2 * ENDS * P * FEATURES_OUT * EDGES
 
@@ -24,7 +26,8 @@ def tile_gather_matmul_kernel(tc, table, w, b, offs, out):
         tc.tile_pool(name="held", bufs=1) as held,
         tc.tile_pool(name="results", bufs=8) as results,
         tc.psum_pool(name="flips", bufs=3) as flips,
-        tc.psum_pool(name="sums", bufs=5) as sums,
+        tc.psum_pool(name="sums", bufs=4) as sums,
+        tc.psum_pool(name="warm", bufs=1) as warm,
     ):
         node_rows = []
         for part in range(n_loads):
@@ -42,6 +45,14 @@ def tile_gather_matmul_kernel(tc, table, w, b, offs, out):
         bias = held.tile([P, FEATURES_OUT // P], F32, name="bias")
         with nc.allow_non_contiguous_dma(reason="one float32 of the bias to a partition"):
             nc.sync.dma_start(bias[:], b.rearrange("(a p) o -> p (a o)", p=P))
+
+        zeros = held.tile([P, P], BF16, name="zeros")
+        nc.gpsimd.memset(zeros[:], 0.0)
+        idle = warm.tile([P, WARM_COLUMNS // P, P], F32, name="idle")
+        for _ in range(WARM_UPS):
+            nc.tensor.matmul(
+                idle[:], zeros[:], zeros[:].unsqueeze(1).to_broadcast([P, WARM_COLUMNS // P, P]), start=True, stop=True
+            )
 
         identity = held.tile([P, P], BF16, name="identity")
         make_identity(nc, identity[:])

@@ -9,7 +9,7 @@ ENDS = 2
 EDGES = 768
 FEATURES_OUT = 256
 PIECE = 384
-HALF = PIECE // 2
+WIDE, NARROW = 256, 128
 PER_COLUMN = 16
 BLOCKS_PER_LOAD = 2
 WARM_UPS = 3
@@ -65,7 +65,7 @@ def tile_gather_matmul_kernel(tc, table, w, b, offs, out):
 
         spans = [(m_block, first_edge, PIECE) for m_block in range(FEATURES_OUT // P) for first_edge in range(0, EDGES, PIECE)]
         last_block, last_first, last_width = spans.pop()
-        spans.extend((last_block, last_first + half * HALF, HALF) for half in range(last_width // HALF))
+        spans.extend([(last_block, last_first, WIDE), (last_block, last_first + WIDE, NARROW)])
 
         n_stores = 0
         for m_block, first_edge, width in spans:
@@ -79,11 +79,12 @@ def tile_gather_matmul_kernel(tc, table, w, b, offs, out):
                     start=(end == 0),
                     stop=(end == ENDS - 1),
                 )
-            for column in range(0, width, HALF):
-                result = results.tile([P, HALF], F32, name="result")
-                nc.vector.tensor_scalar_add(result[:], total[:, column : column + HALF], bias[:, m_block : m_block + 1])
+            for column in range(0, width, WIDE):
+                run = min(WIDE, width - column)
+                result = results.tile([P, WIDE], F32, name="result")
+                nc.vector.tensor_scalar_add(result[:, :run], total[:, column : column + run], bias[:, m_block : m_block + 1])
                 queue = nc.sync if n_stores % 2 == 0 else nc.scalar
                 queue.dma_start(
-                    out[m_block * P : (m_block + 1) * P, first_edge + column : first_edge + column + HALF], result[:]
+                    out[m_block * P : (m_block + 1) * P, first_edge + column : first_edge + column + run], result[:, :run]
                 )
                 n_stores += 1

@@ -40,11 +40,15 @@ def tile_gather_matmul_kernel(tc, table, w, b, offs, out):
             node_rows.append(rows)
         offsets = held.tile([P, ENDS * EDGES // PER_COLUMN], U16, name="offsets")
         nc.sync.dma_start(offsets[:], offs)
-        weights = held.tile([P, ENDS, FEATURES_OUT], BF16, name="weights")
-        nc.scalar.dma_start(weights[:], w.rearrange("t k m -> k t m"))
+        weights = []
+        for m_block in range(FEATURES_OUT // P):
+            block = held.tile([P, ENDS, P], BF16, name="weights%d" % m_block)
+            queue = nc.scalar if m_block % 2 == 0 else nc.sync
+            queue.dma_start(block[:], w[:, :, m_block * P : (m_block + 1) * P].rearrange("t k m -> k t m"))
+            weights.append(block)
         bias = held.tile([P, FEATURES_OUT // P], F32, name="bias")
         with nc.allow_non_contiguous_dma(reason="one float32 of the bias to a partition"):
-            nc.sync.dma_start(bias[:], b.rearrange("(a p) o -> p (a o)", p=P))
+            nc.scalar.dma_start(bias[:], b.rearrange("(a p) o -> p (a o)", p=P))
 
         zeros = held.tile([P, P], BF16, name="zeros")
         nc.gpsimd.memset(zeros[:], 0.0)
@@ -74,7 +78,7 @@ def tile_gather_matmul_kernel(tc, table, w, b, offs, out):
                 first = (end * EDGES + first_edge) // PER_COLUMN
                 nc.tensor.matmul(
                     total[:],
-                    weights[:, end, m_block * P : (m_block + 1) * P],
+                    weights[m_block][:, end, :],
                     window[:].indirect(offsets[:, first : first + width // PER_COLUMN]),
                     start=(end == 0),
                     stop=(end == ENDS - 1),

@@ -51,7 +51,7 @@ def tile_gather_matmul_kernel(tc, table, w, b, offs, out):
             nc.scalar.dma_start(bias[:], b.rearrange("(a p) o -> p (a o)", p=P))
 
         zeros = held.tile([P, P], BF16, name="zeros")
-        nc.gpsimd.memset(zeros[:], 0.0)
+        nc.vector.memset(zeros[:], 0.0)
         idle = warm.tile([P, WARM_COLUMNS // P, P], F32, name="idle")
         for _ in range(WARM_UPS):
             nc.tensor.matmul(

@@ -25,9 +25,8 @@ def tile_gather_matmul_kernel(tc, table, w, b, offs, out):
     with (
         tc.tile_pool(name="held", bufs=1) as held,
         tc.tile_pool(name="results", bufs=8) as results,
-        tc.psum_pool(name="flips", bufs=3) as flips,
+        tc.psum_pool(name="flips", bufs=4) as flips,
         tc.psum_pool(name="sums", bufs=4) as sums,
-        tc.psum_pool(name="warm", bufs=1) as warm,
     ):
         node_rows = []
         for part in range(n_loads):
@@ -50,12 +49,12 @@ def tile_gather_matmul_kernel(tc, table, w, b, offs, out):
         with nc.allow_non_contiguous_dma(reason="one float32 of the bias to a partition"):
             nc.scalar.dma_start(bias[:], b.rearrange("(a p) o -> p (a o)", p=P))
 
-        zeros = held.tile([P, P], BF16, name="zeros")
+        zeros = held.tile([P, 1], BF16, name="zeros")
         nc.vector.memset(zeros[:], 0.0)
-        idle = warm.tile([P, WARM_COLUMNS // P, P], F32, name="idle")
+        idle = sums.tile([P, WARM_COLUMNS], F32, name="idle", tag="total")
         for _ in range(WARM_UPS):
             nc.tensor.matmul(
-                idle[:], zeros[:], zeros[:].unsqueeze(1).to_broadcast([P, WARM_COLUMNS // P, P]), start=True, stop=True
+                idle[:], zeros[:].to_broadcast([P, P]), zeros[:].to_broadcast([P, WARM_COLUMNS]), start=True, stop=True
             )
 
         identity = held.tile([P, P], BF16, name="identity")

@@ -25,10 +25,10 @@ def tile_gather_matmul_kernel(tc, table, w, b, offs, out):
     with (
         tc.tile_pool(name="held", bufs=1) as held,
         tc.tile_pool(name="results", bufs=8) as results,
-        tc.psum_pool(name="flips", bufs=4) as flips,
-        tc.psum_pool(name="sums", bufs=4) as sums,
+        tc.psum_pool(name="flips", bufs=5) as flips,
+        tc.psum_pool(name="sums", bufs=3) as sums,
     ):
-        node_rows = []
+        block_rows = []
         for part in range(n_loads):
             rows = held.tile([P, BLOCKS_PER_LOAD, P], BF16, name="rows%d" % part)
             queue = nc.sync if part % 2 == 0 else nc.scalar
@@ -36,7 +36,7 @@ def tile_gather_matmul_kernel(tc, table, w, b, offs, out):
                 rows[:],
                 table[part * nodes_per_load : (part + 1) * nodes_per_load, :].rearrange("(a p) k -> p a k", p=P),
             )
-            node_rows.append(rows)
+            block_rows.extend([rows[:, a, :] for a in range(BLOCKS_PER_LOAD)])
         offsets = held.tile([P, ENDS * EDGES // PER_COLUMN], U16, name="offsets")
         nc.sync.dma_start(offsets[:], offs)
         weights = []
@@ -60,11 +60,15 @@ def tile_gather_matmul_kernel(tc, table, w, b, offs, out):
         identity = held.tile([P, P], BF16, name="identity")
         make_identity(nc, identity[:])
         window = held.tile([P, NODES], BF16, name="window")
-        for part in range(n_loads):
-            flipped = flips.tile([P, nodes_per_load], BF16, name="flipped")
-            for a in range(BLOCKS_PER_LOAD):
-                nc.tensor.transpose(flipped[:, a * P : (a + 1) * P], node_rows[part][:, a, :], identity[:])
-            nc.vector.tensor_copy(window[:, part * nodes_per_load : (part + 1) * nodes_per_load], flipped[:])
+        first_block = 0
+        for n_blocks in [2] * (NODES // P // 2 - 1) + [1, 1]:
+            flipped = flips.tile([P, 2 * P], BF16, name="flipped")
+            for a in range(n_blocks):
+                nc.tensor.transpose(flipped[:, a * P : (a + 1) * P], block_rows[first_block + a], identity[:])
+            nc.vector.tensor_copy(
+                window[:, first_block * P : (first_block + n_blocks) * P], flipped[:, : n_blocks * P]
+            )
+            first_block += n_blocks
 
         spans = [(m_block, first_edge, PIECE) for m_block in range(FEATURES_OUT // P) for first_edge in range(0, EDGES, PIECE)]
         last_block, last_first, last_width = spans.pop()

import concourse.mybir as mybir
from concourse.masks import make_identity

BF16, F32, U16 = mybir.dt.bfloat16, mybir.dt.float32, mybir.dt.uint16

P = 128
NODES = 1024
ENDS = 2
EDGES = 768
FEATURES_OUT = 256
PIECE = 384
WIDE, NARROW = 256, 128
PER_COLUMN = 16
BLOCKS_PER_LOAD = 2
WARM_UPS = 3
WARM_COLUMNS = 512

FLOPS = 2 * ENDS * P * FEATURES_OUT * EDGES


def tile_gather_matmul_kernel(tc, table, w, b, offs, out):
    nc = tc.nc
    nodes_per_load = BLOCKS_PER_LOAD * P
    n_loads = NODES // nodes_per_load
    with (
        tc.tile_pool(name="held", bufs=1) as held,
        tc.tile_pool(name="results", bufs=8) as results,
        tc.psum_pool(name="flips", bufs=5) as flips,
        tc.psum_pool(name="sums", bufs=3) as sums,
    ):
        block_rows = []
        for part in range(n_loads):
            rows = held.tile([P, BLOCKS_PER_LOAD, P], BF16, name="rows%d" % part)
            queue = nc.sync if part % 2 == 0 else nc.scalar
            queue.dma_start(
                rows[:],
                table[part * nodes_per_load : (part + 1) * nodes_per_load, :].rearrange("(a p) k -> p a k", p=P),
            )
            block_rows.extend([rows[:, a, :] for a in range(BLOCKS_PER_LOAD)])
        offsets = held.tile([P, ENDS * EDGES // PER_COLUMN], U16, name="offsets")
        nc.sync.dma_start(offsets[:], offs)
        weights = []
        for m_block in range(FEATURES_OUT // P):
            block = held.tile([P, ENDS, P], BF16, name="weights%d" % m_block)
            queue = nc.scalar if m_block % 2 == 0 else nc.sync
            queue.dma_start(block[:], w[:, :, m_block * P : (m_block + 1) * P].rearrange("t k m -> k t m"))
            weights.append(block)
        bias = held.tile([P, FEATURES_OUT // P], F32, name="bias")
        with nc.allow_non_contiguous_dma(reason="one float32 of the bias to a partition"):
            nc.scalar.dma_start(bias[:], b.rearrange("(a p) o -> p (a o)", p=P))

        zeros = held.tile([P, 1], BF16, name="zeros")
        nc.vector.memset(zeros[:], 0.0)
        idle = sums.tile([P, WARM_COLUMNS], F32, name="idle", tag="total")
        for _ in range(WARM_UPS):
            nc.tensor.matmul(
                idle[:], zeros[:].to_broadcast([P, P]), zeros[:].to_broadcast([P, WARM_COLUMNS]), start=True, stop=True
            )

        identity = held.tile([P, P], BF16, name="identity")
        make_identity(nc, identity[:])
        window = held.tile([P, NODES], BF16, name="window")
        first_block = 0
        for n_blocks in [2] * (NODES // P // 2 - 1) + [1, 1]:
            flipped = flips.tile([P, 2 * P], BF16, name="flipped")
            for a in range(n_blocks):
                nc.tensor.transpose(flipped[:, a * P : (a + 1) * P], block_rows[first_block + a], identity[:])
            nc.vector.tensor_copy(
                window[:, first_block * P : (first_block + n_blocks) * P], flipped[:, : n_blocks * P]
            )
            first_block += n_blocks

        spans = [(m_block, first_edge, PIECE) for m_block in range(FEATURES_OUT // P) for first_edge in range(0, EDGES, PIECE)]
        last_block, last_first, last_width = spans.pop()
        spans.extend([(last_block, last_first, WIDE), (last_block, last_first + WIDE, NARROW)])

        n_stores = 0
        for m_block, first_edge, width in spans:
            total = sums.tile([P, width], F32, name="total")
            for end in range(ENDS):
                first = (end * EDGES + first_edge) // PER_COLUMN
                nc.tensor.matmul(
                    total[:],
                    weights[m_block][:, end, :],
                    window[:].indirect(offsets[:, first : first + width // PER_COLUMN]),
                    start=(end == 0),
                    stop=(end == ENDS - 1),
                )
            for column in range(0, width, WIDE):
                run = min(WIDE, width - column)
                result = results.tile([P, WIDE], F32, name="result")
                nc.vector.tensor_scalar_add(result[:, :run], total[:, column : column + run], bias[:, m_block : m_block + 1])
                queue = nc.sync if n_stores % 2 == 0 else nc.scalar
                queue.dma_start(
                    out[m_block * P : (m_block + 1) * P, first_edge + column : first_edge + column + run], result[:, :run]
                )
                n_stores += 1
